import numpy as np
import ml_dtypes


def mxq(x, axis, fmt="e4m3"):
    dtype, down = {"e4m3": (ml_dtypes.float8_e4m3fn, 7), "e5m2": (ml_dtypes.float8_e5m2, 14)}[fmt]
    v = np.moveaxis(np.asarray(x, np.float32).astype(ml_dtypes.bfloat16).astype(np.float64), axis, -1)
    blocks = v.reshape(v.shape[:-1] + (-1, 32))
    amax = np.abs(blocks).max(-1, keepdims=True)
    byte = np.maximum(np.where(amax > 0, np.frexp(amax)[1] - 1 + 127, 0) - down, 1)
    scale = np.exp2(byte - 127.0)
    codes = (blocks / scale).astype(np.float32).astype(dtype).astype(np.float64)
    return np.moveaxis((codes * scale).reshape(v.shape), -1, axis)


WIDE = False


def mx_kscale(k):
    if not WIDE:
        return np.ones(k)
    levels = np.array([10, -10, 5, -5, 0])
    if k % 512:
        return np.exp2(np.random.permutation(np.resize(levels, k // 32))).repeat(32)
    a = np.empty((k // 512, 16))
    for p in range(k // 512):
        a[p, :8] = np.random.permutation(np.resize(levels, 8))
        for g in range(8):
            far = levels[np.abs(levels - a[p, g]) >= 10]
            a[p, g + 8] = far[np.random.randint(len(far))]
    return np.exp2(a.ravel()).repeat(32)


def f64(x):
    return np.asarray(x).astype(np.float64)


def striped(idx):
    return np.tile(np.asarray(idx).reshape(-1, 16).T, (8, 1)).astype(np.uint16)


def unstriped(offs):
    return offs[:16].T.reshape(-1).astype(np.int64)


E2M1 = np.array([0.0, 0.5, 1.0, 1.5, 2.0, 3.0, 4.0, 6.0, -0.0, -0.5, -1.0, -1.5, -2.0, -3.0, -4.0, -6.0])


def pack_weight(w, fmt):
    k, n = w.shape
    w = f64(np.asarray(w, np.float32).astype(ml_dtypes.bfloat16)).reshape(k // 32, 32, n)
    amax = np.abs(w).max(1)
    if fmt == "e4m3":
        byte = np.frexp(amax)[1] - 1 + 127 - 7
    else:
        mant, ex = np.frexp(amax / 6.0)
        byte = np.where(mant > 0.5, ex, ex - 1) + 127
    byte = np.clip(np.where(amax > 0, byte, 1), 1, 254)
    scaled = (w * np.exp2(127.0 - byte)[:, None, :]).reshape(k, n).astype(np.float32)
    by_word = np.ascontiguousarray(scaled.reshape(k // 512, 128, 4, n).transpose(0, 1, 3, 2))
    if fmt == "e4m3":
        words = by_word.astype(ml_dtypes.float8_e4m3fn).view(np.uint8)
    else:
        c = by_word.astype(ml_dtypes.float4_e2m1fn).view(np.uint8) & 0xF
        words = (c[..., 0::2] | (c[..., 1::2] << 4)).reshape(k // 512, 128, 2 * n)
    return np.ascontiguousarray(words), np.ascontiguousarray(byte.astype(np.uint8).reshape(k // 512, 16, n))


def unpack_weight(words, scales, fmt):
    g, _, n = scales.shape
    words = np.ascontiguousarray(words).reshape(g, 128, n, -1)
    if fmt == "e4m3":
        vals = words.view(ml_dtypes.float8_e4m3fn).astype(np.float64)
    else:
        nib = np.empty((g, 128, n, 4), np.uint8)
        nib[..., 0::2] = words & 0xF
        nib[..., 1::2] = words >> 4
        vals = E2M1[nib]
    vals = vals * np.repeat(np.exp2(scales.astype(np.float64) - 127.0), 8, axis=1)[..., None]
    return vals.transpose(0, 1, 3, 2).reshape(g * 512, n)


K, L, T, C, V, J = 1024, 512, 256, 2048, 1024, 512


def setup_inputs():
    n = np.random.standard_normal
    idx = np.random.permutation(C)[:J]
    idx2 = np.random.permutation(V)[:J]
    fk = mx_kscale(K)
    fl = mx_kscale(L)
    xtp = pack_weight(n((K, T)) * 0.5 / fk[:, None], "e2m1")
    wcp = pack_weight(n((K, C)) * 1 / np.sqrt(K) * fk[:, None], "e4m3")
    wlp = pack_weight(n((L, V)) * 1 / np.sqrt(L) * fl[:, None], "e2m1")
    return {
        "xt_words": xtp[0],
        "xt_scales": xtp[1],
        "wc_words": wcp[0],
        "wc_scales": wcp[1],
        "xl": (n((L, T)) * 0.5 / fl[:, None]).astype(np.float32),
        "wl_words": wlp[0],
        "wl_scales": wlp[1],
        "offs": striped(idx),
        "offs2": striped(idx2),
    }


def reference(xt_words, xt_scales, wc_words, wc_scales, xl, wl_words, wl_scales, offs, offs2):
    idx = unstriped(offs)
    idx2 = unstriped(offs2)
    xtu = unpack_weight(xt_words, xt_scales, "e2m1")
    wcu = unpack_weight(wc_words, wc_scales, "e4m3")
    wlu = unpack_weight(wl_words, wl_scales, "e2m1")
    wcidxg = wcu[:, idx]
    za = xtu.T @ wcidxg
    xlq = mxq(f64(xl), 0, "e4m3")
    wlidx2g = wlu[:, idx2]
    zb = xlq.T @ wlidx2g
    p = np.exp(za + zb)
    y = 512.0 * p / np.sum(p, axis=1, keepdims=True)
    return y

@@ -1,0 +1,146 @@
+from contextlib import ExitStack
+
+import concourse.mybir as mybir
+
+K, L, T, C, V, J = 1024, 512, 256, 2048, 1024, 512
+FLOPS = 2 * T * J * (K + L)
+
+F32 = mybir.dt.float32
+BF16 = mybir.dt.bfloat16
+I32 = mybir.dt.int32
+U32 = mybir.dt.uint32
+U16 = mybir.dt.uint16
+U8 = mybir.dt.uint8
+FP8X4 = mybir.dt.float8_e4m3fn_x4
+FP4X4 = mybir.dt.float4_e2m1fn_x4
+ALU = mybir.AluOpType
+ACT = mybir.ActivationFunctionType
+
+P = 128
+PACK = 4
+M = 128
+SHIFT = 16
+HALF = J // 2
+NARROW = 128
+
+
+def tile_list_joint_scores_of_two_models_kernel(tc, xt_words, xt_scales, wc_words, wc_scales, xl, wl_words, wl_scales, offs, offs2, out):
+    nc = tc.nc
+    tiles = T // M
+    with ExitStack() as ctx:
+        sb = ctx.enter_context(tc.tile_pool(name="sb", bufs=1))
+        ps = ctx.enter_context(tc.psum_pool(name="ps", bufs=1))
+
+        idx = sb.tile([P, J // 16], U16, name="idx")
+        idx2 = sb.tile([P, J // 16], U16, name="idx2")
+        wcs = sb.tile([P, C], U8, name="wcs", align_bytes=64)
+        wls = sb.tile([P, V], U8, name="wls", align_bytes=64)
+        xts = sb.tile([P, 2, T], U8, name="xts", align_bytes=64)
+        gcs1 = sb.tile([P, J], U8, name="gcs1", align_bytes=64)
+        wlw = sb.tile([P, V], U16, name="wlw", align_bytes=64)
+        wcw = [sb.tile([P, C], I32, name="wcw%d" % z, align_bytes=64) for z in range(2)]
+        xtw = sb.tile([P, 2, 2 * T], U8, name="xtw", align_bytes=64)
+        xlr = sb.tile([P, PACK, T], F32, name="xlr", align_bytes=64)
+
+        nc.vector.memset(wcs[:].bitcast(I32), 0)
+        nc.vector.memset(wls[:].bitcast(I32), 0)
+        nc.vector.memset(xts[:].rearrange("p z t -> p (z t)").bitcast(I32), 0)
+        nc.vector.memset(gcs1[:].bitcast(I32), 0)
+
+        wcs_rows = wc_scales.rearrange("z (q r) c -> r q z c", r=4)
+
+        def load_wcs(eng, r):
+            eng.dma_start(wcs[r:P:SHIFT, :].bitcast(I32), wcs_rows[r].bitcast(I32))
+
+        def load_wcw(z):
+            nc.scalar.dma_start(wcw[z][:], wc_words[z].rearrange("p c r -> p (c r)").bitcast(I32))
+
+        def load_xts(q):
+            nc.sync.dma_start(
+                xts[32 * q : 32 * q + 4, :, :].bitcast(I32),
+                xt_scales[:, 4 * q : 4 * q + 4, :].rearrange("z r t -> r z t").bitcast(I32),
+            )
+
+        nc.sync.dma_start(idx2[:], offs2)
+        nc.sync.dma_start(idx[:], offs)
+        for r in range(2):
+            load_wcs(nc.sync, r)
+        for q in range(4):
+            nc.sync.dma_start(wls[32 * q : 32 * q + 4, :].bitcast(I32), wl_scales[0, 4 * q : 4 * q + 4, :].bitcast(I32))
+
+        nc.scalar.dma_start(wlw[:].bitcast(I32), wl_words[0].bitcast(I32))
+        for r in range(2, 4):
+            load_wcs(nc.scalar, r)
+        load_wcw(0)
+        nc.scalar.dma_start(xlr[:], xl.rearrange("(p j) t -> p j t", j=PACK))
+        nc.scalar.dma_start(xtw[:].bitcast(I32), xt_words.rearrange("z p b -> p z b").bitcast(I32))
+        load_wcw(1)
+
+        glw = sb.tile([P, J], U16, name="glw", align_bytes=64)
+        gcs0 = sb.tile([P, J], U8, name="gcs0", align_bytes=64)
+        gls = sb.tile([P, J], U8, name="gls", align_bytes=64)
+        gcw0 = sb.tile([P, J], I32, name="gcw0", align_bytes=64)
+        gcw1 = [sb.tile([P, HALF], I32, name="gcw1%d" % h, align_bytes=64) for h in range(2)]
+        nc.vector.tensor_copy(glw[:], wlw[:].indirect(idx2[:]))
+        nc.vector.tensor_copy(gcs0[:], wcs[:].indirect(idx[:]))
+        nc.sync.dma_start(gcs1[0 : P - SHIFT, :].bitcast(I32), gcs0[SHIFT:P, :].bitcast(I32))
+        for q in range(4):
+            load_xts(q)
+        nc.vector.tensor_copy(gcw0[:].bitcast(U32), wcw[0][:].bitcast(U32).indirect(idx[:]))
+        nc.vector.tensor_copy(gls[:], wls[:].indirect(idx2[:]))
+
+        xlb = sb.tile([P, T, PACK], BF16, name="xlb", align_bytes=64)
+        nc.scalar.activation(xlb[:], xlr[:].rearrange("p j t -> p t j"), ACT.Copy)
+        xlq = sb.tile([P, T], U32, name="xlq", align_bytes=64)
+        xlqs = sb.tile([P, T], U8, name="xlqs", align_bytes=64)
+        nc.vector.quantize_mx(xlq[:].bitcast(FP8X4), xlqs[:], xlb[:].rearrange("p t j -> p (t j)"))
+
+        for h in range(2):
+            cols = HALF // 16
+            nc.vector.tensor_copy(gcw1[h][:].bitcast(U32), wcw[1][:].bitcast(U32).indirect(idx[:, h * cols : (h + 1) * cols]))
+
+        acc = [ps.tile([M, J], F32, name="acc%d" % m) for m in range(tiles)]
+
+        def xt_operand(m, z):
+            return xtw[:, z, 2 * m * M : 2 * (m + 1) * M].bitcast(FP4X4), xts[:, z, m * M : (m + 1) * M]
+
+        for m in range(tiles):
+            words, scales = xt_operand(m, 0)
+            nc.tensor.matmul_mx(acc[m][:], lhsT=words, lhsT_scale=scales, rhs=gcw0[:].bitcast(FP8X4), rhs_scale=gcs0[:], start=True, stop=False)
+        for m in range(tiles):
+            nc.tensor.matmul_mx(
+                acc[m][:],
+                lhsT=xlq[:, m * M : (m + 1) * M].bitcast(FP8X4),
+                lhsT_scale=xlqs[:, m * M : (m + 1) * M],
+                rhs=glw[:].bitcast(FP4X4),
+                rhs_scale=gls[:],
+                start=False,
+                stop=False,
+            )
+        for h in range(2):
+            for m in range(tiles):
+                words, scales = xt_operand(m, 1)
+                for n in range(0, HALF, NARROW):
+                    j0 = h * HALF + n
+                    nc.tensor.matmul_mx(
+                        acc[m][:, j0 : j0 + NARROW],
+                        lhsT=words,
+                        lhsT_scale=scales,
+                        rhs=gcw1[h][:, n : n + NARROW].bitcast(FP8X4),
+                        rhs_scale=gcs1[:, j0 : j0 + NARROW],
+                        start=False,
+                        stop=(j0 + NARROW == J),
+                    )
+
+        negmax = [sb.tile([P, 1], F32, name="negmax%d" % m) for m in range(tiles)]
+        total = [sb.tile([P, 1], F32, name="total%d" % m) for m in range(tiles)]
+        prob = [sb.tile([P, J], F32, name="prob%d" % m) for m in range(tiles)]
+        for m in range(tiles):
+            nc.vector.tensor_reduce(negmax[m][:], acc[m][:], mybir.AxisListType.X, ALU.max, negate=True)
+            nc.scalar.activation(prob[m][:], acc[m][:], ACT.Exp, bias=negmax[m][:], accum_out=total[m][:])
+        for m in range(tiles):
+            inv = sb.tile([P, 1], F32, name="inv%d" % m)
+            nc.vector.reciprocal(inv[:], total[m][:])
+            res = sb.tile([P, J], F32, name="res%d" % m)
+            nc.vector.tensor_scalar(res[:], prob[m][:], inv[:], float(J), ALU.mult, ALU.mult)
+            nc.sync.dma_start(out[m * M : (m + 1) * M, :], res[:])

@@ -33,7 +33,7 @@ def tile_list_joint_scores_of_two_models_kernel(tc, xt_words, xt_scales, wc_word
 
         idx = sb.tile([P, J // 16], U16, name="idx")
         idx2 = sb.tile([P, J // 16], U16, name="idx2")
-        wcs = sb.tile([P, C], U8, name="wcs", align_bytes=64)
+        wcs = sb.tile([P, C], U8, name="wcs", tag="wcs_slot", align_bytes=64)
         wls = sb.tile([P, V], U8, name="wls", align_bytes=64)
         xts = sb.tile([P, 2, T], U8, name="xts", align_bytes=64)
         gcs1 = sb.tile([P, J], U8, name="gcs1", align_bytes=64)
@@ -44,7 +44,7 @@ def tile_list_joint_scores_of_two_models_kernel(tc, xt_words, xt_scales, wc_word
 
         nc.vector.memset(wcs[:].bitcast(I32), 0)
         nc.vector.memset(wls[:].bitcast(I32), 0)
-        nc.vector.memset(xts[:].rearrange("p z t -> p (z t)").bitcast(I32), 0)
+        nc.gpsimd.memset(xts[:].rearrange("p z t -> p (z t)").bitcast(I32), 0)
         nc.vector.memset(gcs1[:].bitcast(I32), 0)
 
         wcs_rows = wc_scales.rearrange("z (q r) c -> r q z c", r=4)
@@ -56,31 +56,28 @@ def tile_list_joint_scores_of_two_models_kernel(tc, xt_words, xt_scales, wc_word
             nc.scalar.dma_start(wcw[z][:], wc_words[z].rearrange("p c r -> p (c r)").bitcast(I32))
 
         def load_xts(q):
-            nc.sync.dma_start(
+            nc.gpsimd.dma_start(
                 xts[32 * q : 32 * q + 4, :, :].bitcast(I32),
                 xt_scales[:, 4 * q : 4 * q + 4, :].rearrange("z r t -> r z t").bitcast(I32),
             )
 
         nc.sync.dma_start(idx2[:], offs2)
         nc.sync.dma_start(idx[:], offs)
-        for r in range(2):
+        for r in range(4):
             load_wcs(nc.sync, r)
         for q in range(4):
             nc.sync.dma_start(wls[32 * q : 32 * q + 4, :].bitcast(I32), wl_scales[0, 4 * q : 4 * q + 4, :].bitcast(I32))
 
         nc.scalar.dma_start(wlw[:].bitcast(I32), wl_words[0].bitcast(I32))
-        for r in range(2, 4):
-            load_wcs(nc.scalar, r)
         load_wcw(0)
-        nc.scalar.dma_start(xlr[:], xl.rearrange("(p j) t -> p j t", j=PACK))
         nc.scalar.dma_start(xtw[:].bitcast(I32), xt_words.rearrange("z p b -> p z b").bitcast(I32))
+        nc.scalar.dma_start(xlr[:], xl.rearrange("(p j) t -> p j t", j=PACK))
         load_wcw(1)
 
         glw = sb.tile([P, J], U16, name="glw", align_bytes=64)
         gcs0 = sb.tile([P, J], U8, name="gcs0", align_bytes=64)
         gls = sb.tile([P, J], U8, name="gls", align_bytes=64)
-        gcw0 = sb.tile([P, J], I32, name="gcw0", align_bytes=64)
-        gcw1 = [sb.tile([P, HALF], I32, name="gcw1%d" % h, align_bytes=64) for h in range(2)]
+        gcw0 = sb.tile([P, J], I32, name="gcw0", tag="wcs_slot", align_bytes=64)
         nc.vector.tensor_copy(glw[:], wlw[:].indirect(idx2[:]))
         nc.vector.tensor_copy(gcs0[:], wcs[:].indirect(idx[:]))
         nc.sync.dma_start(gcs1[0 : P - SHIFT, :].bitcast(I32), gcs0[SHIFT:P, :].bitcast(I32))
@@ -89,15 +86,16 @@ def tile_list_joint_scores_of_two_models_kernel(tc, xt_words, xt_scales, wc_word
         nc.vector.tensor_copy(gcw0[:].bitcast(U32), wcw[0][:].bitcast(U32).indirect(idx[:]))
         nc.vector.tensor_copy(gls[:], wls[:].indirect(idx2[:]))
 
-        xlb = sb.tile([P, T, PACK], BF16, name="xlb", align_bytes=64)
+        xlb = sb.tile([P, T, PACK], BF16, name="xlb", tag="xlb_slot", align_bytes=64)
         nc.scalar.activation(xlb[:], xlr[:].rearrange("p j t -> p t j"), ACT.Copy)
         xlq = sb.tile([P, T], U32, name="xlq", align_bytes=64)
         xlqs = sb.tile([P, T], U8, name="xlqs", align_bytes=64)
         nc.vector.quantize_mx(xlq[:].bitcast(FP8X4), xlqs[:], xlb[:].rearrange("p t j -> p (t j)"))
 
+        gcw1 = sb.tile([P, J], I32, name="gcw1", tag="xlb_slot", align_bytes=64)
         for h in range(2):
             cols = HALF // 16
-            nc.vector.tensor_copy(gcw1[h][:].bitcast(U32), wcw[1][:].bitcast(U32).indirect(idx[:, h * cols : (h + 1) * cols]))
+            nc.vector.tensor_copy(gcw1[:, h * HALF : (h + 1) * HALF].bitcast(U32), wcw[1][:].bitcast(U32).indirect(idx[:, h * cols : (h + 1) * cols]))
 
         acc = [ps.tile([M, J], F32, name="acc%d" % m) for m in range(tiles)]
 
@@ -126,7 +124,7 @@ def tile_list_joint_scores_of_two_models_kernel(tc, xt_words, xt_scales, wc_word
                         acc[m][:, j0 : j0 + NARROW],
                         lhsT=words,
                         lhsT_scale=scales,
-                        rhs=gcw1[h][:, n : n + NARROW].bitcast(FP8X4),
+                        rhs=gcw1[:, j0 : j0 + NARROW].bitcast(FP8X4),
                         rhs_scale=gcs1[:, j0 : j0 + NARROW],
                         start=False,
                         stop=(j0 + NARROW == J),
@@ -142,5 +140,7 @@ def tile_list_joint_scores_of_two_models_kernel(tc, xt_words, xt_scales, wc_word
             inv = sb.tile([P, 1], F32, name="inv%d" % m)
             nc.vector.reciprocal(inv[:], total[m][:])
             res = sb.tile([P, J], F32, name="res%d" % m)
-            nc.vector.tensor_scalar(res[:], prob[m][:], inv[:], float(J), ALU.mult, ALU.mult)
-            nc.sync.dma_start(out[m * M : (m + 1) * M, :], res[:])
+            parts = [(0, J, nc.sync)] if m < tiles - 1 else [(0, HALF, nc.sync), (HALF, J, nc.scalar)]
+            for lo, hi, queue in parts:
+                nc.vector.tensor_scalar(res[:, lo:hi], prob[m][:, lo:hi], inv[:], float(J), ALU.mult, ALU.mult)
+                queue.dma_start(out[m * M : (m + 1) * M, lo:hi], res[:, lo:hi])

@@ -33,7 +33,7 @@ def tile_list_joint_scores_of_two_models_kernel(tc, xt_words, xt_scales, wc_word
 
         idx = sb.tile([P, J // 16], U16, name="idx")
         idx2 = sb.tile([P, J // 16], U16, name="idx2")
-        wcs = sb.tile([P, C], U8, name="wcs", tag="wcs_slot", align_bytes=64)
+        wcs = sb.tile([P, C], U8, name="wcs", align_bytes=64)
         wls = sb.tile([P, V], U8, name="wls", align_bytes=64)
         xts = sb.tile([P, 2, T], U8, name="xts", align_bytes=64)
         gcs1 = sb.tile([P, J], U8, name="gcs1", align_bytes=64)
@@ -43,59 +43,54 @@ def tile_list_joint_scores_of_two_models_kernel(tc, xt_words, xt_scales, wc_word
         xlr = sb.tile([P, PACK, T], F32, name="xlr", align_bytes=64)
 
         nc.vector.memset(wcs[:].bitcast(I32), 0)
-        nc.vector.memset(wls[:].bitcast(I32), 0)
         nc.gpsimd.memset(xts[:].rearrange("p z t -> p (z t)").bitcast(I32), 0)
+        nc.vector.memset(wls[:].bitcast(I32), 0)
         nc.vector.memset(gcs1[:].bitcast(I32), 0)
 
         wcs_rows = wc_scales.rearrange("z (q r) c -> r q z c", r=4)
-
-        def load_wcs(eng, r):
-            eng.dma_start(wcs[r:P:SHIFT, :].bitcast(I32), wcs_rows[r].bitcast(I32))
+        wls_rows = wl_scales[0].rearrange("(q r) v -> r q v", r=4)
+        xts_rows = xt_scales.rearrange("z (q r) t -> r q z t", r=4)
 
         def load_wcw(z):
-            nc.scalar.dma_start(wcw[z][:], wc_words[z].rearrange("p c r -> p (c r)").bitcast(I32))
+            nc.sync.dma_start(wcw[z][:], wc_words[z].rearrange("p c r -> p (c r)").bitcast(I32))
 
-        def load_xts(q):
-            nc.gpsimd.dma_start(
-                xts[32 * q : 32 * q + 4, :, :].bitcast(I32),
-                xt_scales[:, 4 * q : 4 * q + 4, :].rearrange("z r t -> r z t").bitcast(I32),
-            )
-
+        for r in range(4):
+            nc.gpsimd.dma_start(xts[r:P:32, :, :].bitcast(I32), xts_rows[r].bitcast(I32))
         nc.sync.dma_start(idx2[:], offs2)
         nc.sync.dma_start(idx[:], offs)
-        for r in range(4):
-            load_wcs(nc.sync, r)
-        for q in range(4):
-            nc.sync.dma_start(wls[32 * q : 32 * q + 4, :].bitcast(I32), wl_scales[0, 4 * q : 4 * q + 4, :].bitcast(I32))
-
         nc.scalar.dma_start(wlw[:].bitcast(I32), wl_words[0].bitcast(I32))
+        for r in range(4):
+            queue = nc.sync if r < 2 else nc.scalar
+            queue.dma_start(wcs[r:P:SHIFT, :].bitcast(I32), wcs_rows[r].bitcast(I32))
         load_wcw(0)
-        nc.scalar.dma_start(xtw[:].bitcast(I32), xt_words.rearrange("z p b -> p z b").bitcast(I32))
-        nc.scalar.dma_start(xlr[:], xl.rearrange("(p j) t -> p j t", j=PACK))
+        for r in range(4):
+            nc.sync.dma_start(wls[r:P:32, :].bitcast(I32), wls_rows[r].bitcast(I32))
+        nc.sync.dma_start(xlr[:], xl.rearrange("(p j) t -> p j t", j=PACK))
+        nc.sync.dma_start(xtw[:].bitcast(I32), xt_words.rearrange("z p b -> p z b").bitcast(I32))
         load_wcw(1)
 
         glw = sb.tile([P, J], U16, name="glw", align_bytes=64)
         gcs0 = sb.tile([P, J], U8, name="gcs0", align_bytes=64)
         gls = sb.tile([P, J], U8, name="gls", align_bytes=64)
-        gcw0 = sb.tile([P, J], I32, name="gcw0", tag="wcs_slot", align_bytes=64)
+        gcw0 = sb.tile([P, J], I32, name="gcw0", align_bytes=64)
+        gcw1 = [sb.tile([P, HALF], I32, name="gcw1%d" % h, align_bytes=64) for h in range(2)]
         nc.vector.tensor_copy(glw[:], wlw[:].indirect(idx2[:]))
         nc.vector.tensor_copy(gcs0[:], wcs[:].indirect(idx[:]))
         nc.sync.dma_start(gcs1[0 : P - SHIFT, :].bitcast(I32), gcs0[SHIFT:P, :].bitcast(I32))
-        for q in range(4):
-            load_xts(q)
         nc.vector.tensor_copy(gcw0[:].bitcast(U32), wcw[0][:].bitcast(U32).indirect(idx[:]))
         nc.vector.tensor_copy(gls[:], wls[:].indirect(idx2[:]))
 
-        xlb = sb.tile([P, T, PACK], BF16, name="xlb", tag="xlb_slot", align_bytes=64)
-        nc.scalar.activation(xlb[:], xlr[:].rearrange("p j t -> p t j"), ACT.Copy)
-        xlq = sb.tile([P, T], U32, name="xlq", align_bytes=64)
-        xlqs = sb.tile([P, T], U8, name="xlqs", align_bytes=64)
-        nc.vector.quantize_mx(xlq[:].bitcast(FP8X4), xlqs[:], xlb[:].rearrange("p t j -> p (t j)"))
+        xlb = [sb.tile([P, M, PACK], BF16, name="xlb%d" % m, align_bytes=64) for m in range(tiles)]
+        xlq = [sb.tile([P, M], U32, name="xlq%d" % m, align_bytes=64) for m in range(tiles)]
+        xlqs = [sb.tile([P, M], U8, name="xlqs%d" % m, align_bytes=64) for m in range(tiles)]
+        nc.vector.tensor_copy(xlb[0][:], xlr[:, :, 0:M].rearrange("p j t -> p t j"))
+        nc.scalar.activation(xlb[1][:], xlr[:, :, M:T].rearrange("p j t -> p t j"), ACT.Copy)
+        for m in range(tiles):
+            nc.vector.quantize_mx(xlq[m][:].bitcast(FP8X4), xlqs[m][:], xlb[m][:].rearrange("p t j -> p (t j)"))
 
-        gcw1 = sb.tile([P, J], I32, name="gcw1", tag="xlb_slot", align_bytes=64)
         for h in range(2):
             cols = HALF // 16
-            nc.vector.tensor_copy(gcw1[:, h * HALF : (h + 1) * HALF].bitcast(U32), wcw[1][:].bitcast(U32).indirect(idx[:, h * cols : (h + 1) * cols]))
+            nc.vector.tensor_copy(gcw1[h][:].bitcast(U32), wcw[1][:].bitcast(U32).indirect(idx[:, h * cols : (h + 1) * cols]))
 
         acc = [ps.tile([M, J], F32, name="acc%d" % m) for m in range(tiles)]
 
@@ -108,8 +103,8 @@ def tile_list_joint_scores_of_two_models_kernel(tc, xt_words, xt_scales, wc_word
         for m in range(tiles):
             nc.tensor.matmul_mx(
                 acc[m][:],
-                lhsT=xlq[:, m * M : (m + 1) * M].bitcast(FP8X4),
-                lhsT_scale=xlqs[:, m * M : (m + 1) * M],
+                lhsT=xlq[m][:].bitcast(FP8X4),
+                lhsT_scale=xlqs[m][:],
                 rhs=glw[:].bitcast(FP4X4),
                 rhs_scale=gls[:],
                 start=False,
@@ -124,7 +119,7 @@ def tile_list_joint_scores_of_two_models_kernel(tc, xt_words, xt_scales, wc_word
                         acc[m][:, j0 : j0 + NARROW],
                         lhsT=words,
                         lhsT_scale=scales,
-                        rhs=gcw1[:, j0 : j0 + NARROW].bitcast(FP8X4),
+                        rhs=gcw1[h][:, n : n + NARROW].bitcast(FP8X4),
                         rhs_scale=gcs1[:, j0 : j0 + NARROW],
                         start=False,
                         stop=(j0 + NARROW == J),

from contextlib import ExitStack

import concourse.mybir as mybir

K, L, T, C, V, J = 1024, 512, 256, 2048, 1024, 512
FLOPS = 2 * T * J * (K + L)

F32 = mybir.dt.float32
BF16 = mybir.dt.bfloat16
I32 = mybir.dt.int32
U32 = mybir.dt.uint32
U16 = mybir.dt.uint16
U8 = mybir.dt.uint8
FP8X4 = mybir.dt.float8_e4m3fn_x4
FP4X4 = mybir.dt.float4_e2m1fn_x4
ALU = mybir.AluOpType
ACT = mybir.ActivationFunctionType

P = 128
PACK = 4
M = 128
SHIFT = 16
HALF = J // 2
NARROW = 128


def tile_list_joint_scores_of_two_models_kernel(tc, xt_words, xt_scales, wc_words, wc_scales, xl, wl_words, wl_scales, offs, offs2, out):
    nc = tc.nc
    tiles = T // M
    with ExitStack() as ctx:
        sb = ctx.enter_context(tc.tile_pool(name="sb", bufs=1))
        ps = ctx.enter_context(tc.psum_pool(name="ps", bufs=1))

        idx = sb.tile([P, J // 16], U16, name="idx")
        idx2 = sb.tile([P, J // 16], U16, name="idx2")
        wcs = sb.tile([P, C], U8, name="wcs", align_bytes=64)
        wls = sb.tile([P, V], U8, name="wls", align_bytes=64)
        xts = sb.tile([P, 2, T], U8, name="xts", align_bytes=64)
        gcs1 = sb.tile([P, J], U8, name="gcs1", align_bytes=64)
        wlw = sb.tile([P, V], U16, name="wlw", align_bytes=64)
        wcw = [sb.tile([P, C], I32, name="wcw%d" % z, align_bytes=64) for z in range(2)]
        xtw = sb.tile([P, 2, 2 * T], U8, name="xtw", align_bytes=64)
        xlr = sb.tile([P, PACK, T], F32, name="xlr", align_bytes=64)

        nc.vector.memset(wcs[:].bitcast(I32), 0)
        nc.gpsimd.memset(xts[:].rearrange("p z t -> p (z t)").bitcast(I32), 0)
        nc.vector.memset(wls[:].bitcast(I32), 0)
        nc.vector.memset(gcs1[:].bitcast(I32), 0)

        wcs_rows = wc_scales.rearrange("z (q r) c -> r q z c", r=4)
        wls_rows = wl_scales[0].rearrange("(q r) v -> r q v", r=4)
        xts_rows = xt_scales.rearrange("z (q r) t -> r q z t", r=4)

        def load_wcw(z):
            nc.sync.dma_start(wcw[z][:], wc_words[z].rearrange("p c r -> p (c r)").bitcast(I32))

        for r in range(4):
            nc.gpsimd.dma_start(xts[r:P:32, :, :].bitcast(I32), xts_rows[r].bitcast(I32))
        nc.sync.dma_start(idx2[:], offs2)
        nc.sync.dma_start(idx[:], offs)
        nc.scalar.dma_start(wlw[:].bitcast(I32), wl_words[0].bitcast(I32))
        for r in range(4):
            queue = nc.sync if r < 2 else nc.scalar
            queue.dma_start(wcs[r:P:SHIFT, :].bitcast(I32), wcs_rows[r].bitcast(I32))
        load_wcw(0)
        for r in range(4):
            nc.sync.dma_start(wls[r:P:32, :].bitcast(I32), wls_rows[r].bitcast(I32))
        nc.sync.dma_start(xlr[:], xl.rearrange("(p j) t -> p j t", j=PACK))
        nc.sync.dma_start(xtw[:].bitcast(I32), xt_words.rearrange("z p b -> p z b").bitcast(I32))
        load_wcw(1)

        glw = sb.tile([P, J], U16, name="glw", align_bytes=64)
        gcs0 = sb.tile([P, J], U8, name="gcs0", align_bytes=64)
        gls = sb.tile([P, J], U8, name="gls", align_bytes=64)
        gcw0 = sb.tile([P, J], I32, name="gcw0", align_bytes=64)
        gcw1 = [sb.tile([P, HALF], I32, name="gcw1%d" % h, align_bytes=64) for h in range(2)]
        nc.vector.tensor_copy(glw[:], wlw[:].indirect(idx2[:]))
        nc.vector.tensor_copy(gcs0[:], wcs[:].indirect(idx[:]))
        nc.sync.dma_start(gcs1[0 : P - SHIFT, :].bitcast(I32), gcs0[SHIFT:P, :].bitcast(I32))
        nc.vector.tensor_copy(gcw0[:].bitcast(U32), wcw[0][:].bitcast(U32).indirect(idx[:]))
        nc.vector.tensor_copy(gls[:], wls[:].indirect(idx2[:]))

        xlb = [sb.tile([P, M, PACK], BF16, name="xlb%d" % m, align_bytes=64) for m in range(tiles)]
        xlq = [sb.tile([P, M], U32, name="xlq%d" % m, align_bytes=64) for m in range(tiles)]
        xlqs = [sb.tile([P, M], U8, name="xlqs%d" % m, align_bytes=64) for m in range(tiles)]
        nc.vector.tensor_copy(xlb[0][:], xlr[:, :, 0:M].rearrange("p j t -> p t j"))
        nc.scalar.activation(xlb[1][:], xlr[:, :, M:T].rearrange("p j t -> p t j"), ACT.Copy)
        for m in range(tiles):
            nc.vector.quantize_mx(xlq[m][:].bitcast(FP8X4), xlqs[m][:], xlb[m][:].rearrange("p t j -> p (t j)"))

        for h in range(2):
            cols = HALF // 16
            nc.vector.tensor_copy(gcw1[h][:].bitcast(U32), wcw[1][:].bitcast(U32).indirect(idx[:, h * cols : (h + 1) * cols]))

        acc = [ps.tile([M, J], F32, name="acc%d" % m) for m in range(tiles)]

        def xt_operand(m, z):
            return xtw[:, z, 2 * m * M : 2 * (m + 1) * M].bitcast(FP4X4), xts[:, z, m * M : (m + 1) * M]

        for m in range(tiles):
            words, scales = xt_operand(m, 0)
            nc.tensor.matmul_mx(acc[m][:], lhsT=words, lhsT_scale=scales, rhs=gcw0[:].bitcast(FP8X4), rhs_scale=gcs0[:], start=True, stop=False)
        for m in range(tiles):
            nc.tensor.matmul_mx(
                acc[m][:],
                lhsT=xlq[m][:].bitcast(FP8X4),
                lhsT_scale=xlqs[m][:],
                rhs=glw[:].bitcast(FP4X4),
                rhs_scale=gls[:],
                start=False,
                stop=False,
            )
        for h in range(2):
            for m in range(tiles):
                words, scales = xt_operand(m, 1)
                for n in range(0, HALF, NARROW):
                    j0 = h * HALF + n
                    nc.tensor.matmul_mx(
                        acc[m][:, j0 : j0 + NARROW],
                        lhsT=words,
                        lhsT_scale=scales,
                        rhs=gcw1[h][:, n : n + NARROW].bitcast(FP8X4),
                        rhs_scale=gcs1[:, j0 : j0 + NARROW],
                        start=False,
                        stop=(j0 + NARROW == J),
                    )

        negmax = [sb.tile([P, 1], F32, name="negmax%d" % m) for m in range(tiles)]
        total = [sb.tile([P, 1], F32, name="total%d" % m) for m in range(tiles)]
        prob = [sb.tile([P, J], F32, name="prob%d" % m) for m in range(tiles)]
        for m in range(tiles):
            nc.vector.tensor_reduce(negmax[m][:], acc[m][:], mybir.AxisListType.X, ALU.max, negate=True)
            nc.scalar.activation(prob[m][:], acc[m][:], ACT.Exp, bias=negmax[m][:], accum_out=total[m][:])
        for m in range(tiles):
            inv = sb.tile([P, 1], F32, name="inv%d" % m)
            nc.vector.reciprocal(inv[:], total[m][:])
            res = sb.tile([P, J], F32, name="res%d" % m)
            parts = [(0, J, nc.sync)] if m < tiles - 1 else [(0, HALF, nc.sync), (HALF, J, nc.scalar)]
            for lo, hi, queue in parts:
                nc.vector.tensor_scalar(res[:, lo:hi], prob[m][:, lo:hi], inv[:], float(J), ALU.mult, ALU.mult)
                queue.dma_start(out[m * M : (m + 1) * M, lo:hi], res[:, lo:hi])
